import numpy as np, ml_dtypes
CORES = [51,54,179,182]
N = 4
import mx_ref
BF = ml_dtypes.bfloat16
def entries(a):
    return np.ascontiguousarray(a.T).reshape(-1)
def table(e):
    return np.ascontiguousarray(np.reshape(e, (-1, 16)).T).astype(np.int32)
def cols(t, e):
    v = np.concatenate([t.reshape(128, -1, 4), np.zeros((128, 1, 4), BF)], axis=1)
    return np.ascontiguousarray(v[:, e]).reshape(128, -1)
def cut(t, i, w=512):
    return t[:, w * i:w * i + w]
def f(rng, *shape):
    return mx_ref.flush((rng.standard_normal(shape, dtype=np.float32) * np.exp2(rng.integers(-2, 3, shape[:-1] + (1,)))).astype(BF))
def wide(rng, *shape, cols=0):
    v = rng.standard_normal(shape, dtype=np.float32) * np.exp2(rng.integers(-12, 13, shape)).astype(np.float32)
    if cols: v *= np.repeat(np.exp2(rng.integers(-cols, cols + 1, shape[:-2] + (1, shape[-1] // 4))) * (rng.random(shape[:-2] + (1, shape[-1] // 4)) > 0.0625), 4, axis=-1).astype(np.float32)
    return mx_ref.flush(v.astype(BF))
T, K, O, CAPP = 512, 8, 1, 96
def lists(rng, foreign=False, own=False, same=False, absent=False):
    S = np.full((N, N, CAPP), -1); M = []
    for s in range(N):
        for d in range(N):
            n = CAPP if foreign else rng.integers(1, CAPP + 1)
            if s != d: S[s, d, rng.permutation(CAPP)[:n]] = rng.integers(0, T, n)
    k = np.arange(K)[:, None]
    for r in range(N):
        far = T + np.flatnonzero(S[:, r].reshape(-1) >= 0)
        m = np.where(rng.random((K, T)) < (1.0 if foreign else np.divide(k + 1, K + 1)), rng.choice(far, (K, T)), rng.integers(0, T, (K, T)))
        there = np.zeros((K, T), bool); there[rng.integers(0, K, T), np.arange(T)] = True
        if absent: there.reshape(-1)[rng.permutation(np.flatnonzero(~there))[:K * T - 2 * K * T // 3 - T]] = True
        else: there |= rng.random((K, T)) >= 0.1 + 0.5 * np.divide(k, K - 1)
        m = np.repeat(m[:, :1], T, axis=1) if same else np.where(there, m, -1)
        if own: m = np.stack([rng.permutation(T) for _ in range(K)])
        M.append(table(m))
    return {"send": np.stack([table(S[s]) for s in range(N)]), "mp": np.stack(M)}
def setup_inputs(rng):
    return {"x": f(rng, N, 128, 4 * T), "w": f(rng, N, 128, K * O * 512), **lists(rng)}
def setup_inputs_absent(rng):
    return {**setup_inputs(rng), **lists(rng, absent=True)}
def setup_inputs_foreign(rng):
    return {**setup_inputs(rng), **lists(rng, foreign=True)}
def setup_inputs_same(rng):
    return {**setup_inputs(rng), **lists(rng, same=True)}
def setup_inputs_spread(rng):
    d = setup_inputs(rng); d["x"] = wide(rng, N, 128, 4 * T); return d
def setup_inputs_own(rng):
    return {**setup_inputs(rng), **lists(rng, own=True)}
def check_inputs(d):
    b = []
    for n in ("x", "w"):
        a = np.abs(d[n].astype(np.float32))
        if not np.isfinite(a).all() or ((a > 0) & ((a < 2.0 ** -30) | (a > 2.0 ** 30))).any(): b.append(n)
    for r in range(N):
        s, m = entries(d["send"][r]), entries(d["mp"][r]).reshape(K, T)
        if s.min() < -1 or s.max() >= T or (s[r * CAPP:(r + 1) * CAPP] != -1).any(): b.append("send")
        held = np.concatenate([entries(d["send"][q])[r * CAPP:(r + 1) * CAPP] for q in range(N)])
        if m.min() < -1 or m.max() >= T + N * CAPP or (held[m[m >= T] - T] < 0).any() or (m < 0).all(axis=0).any(): b.append("mp")
    return b
def reference(x, w, send, mp):
    y = np.zeros((N, 128, O * T), np.float32)
    for r in range(N):
        held = [cols(x[s], entries(send[s])[r * CAPP:(r + 1) * CAPP]) for s in range(N)]
        v = np.concatenate([x[r]] + held, axis=1)
        m = entries(mp[r]).reshape(K, T)
        for k in range(K):
            q = mx_ref.quantize(cols(v, m[k]))
            for o in range(O): y[r][:, T * o:T * o + T] += mx_ref.matmul(mx_ref.quantize(cut(w[r], k * O + o)), q)
    return {"y": y}

@@ -1,0 +1,224 @@
+from concourse.bass import DstId, RemoteDMATransfer
+from concourse.mybir import dt, AluOpType, ActivationFunctionType
+
+COLS, MAPS, CAPP, N = 512, 8, 96, 4
+WIN = 1 + COLS + N * CAPP
+NEAR0, FAR0 = COLS, COLS + CAPP
+CUT = [(0, 256), (256, 416), (416, 512)]
+VM = [[1, 3, 5, 7], [1, 7], [1, 7]]
+EVV = [1, 3, 5, 7]
+NE = 8
+
+SCRATCH = {
+    "xs": ("sbuf", [128, 4 * COLS], "bfloat16"),
+    "wt": ("sbuf", [128, 512 * MAPS], "bfloat16"),
+    "sl": ("sbuf", [32, N * CAPP // 16], "int32"),
+    "so": ("sbuf", [128, N * CAPP // 16], "uint16"),
+    "ml": ("sbuf", [128, MAPS * COLS // 16], "int32"),
+    "mo": ("sbuf", [128, MAPS * COLS // 16], "uint16"),
+    "h": ("sbuf", [128, 4 * 3 * CAPP], "bfloat16"),
+    "hq": ("sbuf", [128, 2 * CAPP], "float8_e4m3fn_x4"),
+    "hs": ("sbuf", [128, 2 * CAPP], "uint8"),
+    "nq": ("sbuf", [128, 128], "float8_e4m3fn_x4"),
+    "ns": ("sbuf", [128, 128], "uint8"),
+    "qf": ("sbuf", [128, COLS + 3 * CAPP], "float8_e4m3fn_x4"),
+    "sf": ("sbuf", [128, COLS + 3 * CAPP], "uint8"),
+    "qw": ("sbuf", [128, 128 * MAPS], "float8_e4m3fn_x4"),
+    "sw": ("sbuf", [128, 128 * MAPS], "uint8"),
+    "win": ("sbuf", [128, MAPS * WIN], "float32"),
+    "gs": ("sbuf", [128, 3 * COLS], "float32"),
+    "pq": ("sbuf", [128, 8 * COLS], "float32"),
+    "zz": ("sbuf", [128, 8 * COLS], "float32"),
+    "ys": ("sbuf", [128, COLS], "float32"),
+    "ps": ("psum", [128, 512 * MAPS], "float32"),
+}
+for _v in VM:
+    SCRATCH["one%d" % (MAPS - len(_v))] = ("sbuf", [128, 1024], "bfloat16")
+SEMAPHORES = ["v", "s", "t", "dx", "dl", "dw0", "dw1", "dw2", "dw3", "dm", "dy", "near", "far", "gone"]
+
+
+def rank_program(g, core, T, topo):
+    r = T.rank_of(core)
+    if r is None:
+        return
+    cores = list(T.cores)
+
+    def near_of(d):
+        return [s for s in range(N) if s != d and cores[s] in topo.cores_of(cores[d])]
+
+    def far_of(d):
+        return [s for s in range(N) if cores[s] not in topo.cores_of(cores[d])]
+
+    near, far = near_of(r)[0], far_of(r)
+    Copy, add = ActivationFunctionType.Copy, AluOpType.add
+
+    queue = {"v": g.vector, "s": g.scalar, "t": g.tensor, "y": g.sync, "g": g}
+    count, seen = {}, {}
+
+    def wait(q, deps):
+        for sem, n in deps:
+            if seen.get((q, sem), 0) < n:
+                queue[q].wait_ge(T.sem[sem], n)
+                seen[(q, sem)] = n
+
+    def run(q, deps, call, sem=None, n=1):
+        wait(q, deps)
+        sem = sem or q
+        call(queue[q]).then_inc(T.sem[sem], n)
+        count[sem] = count.get(sem, 0) + n
+        return (sem, count[sem])
+
+    run("y", [], lambda q: q.dma_start(T.xs[0:32, :], T.x[0:32, :]), "dx", 16)
+    run("s", [], lambda q: q.dma_start(T.sl[0:16, :], T.send[:]), "dl", 16)
+    lx = run("y", [], lambda q: q.dma_start(T.xs[32:128, :], T.x[32:128, :]), "dx", 16)
+    ll = run("s", [], lambda q: q.dma_start(T.sl[16:32, :], T.send[:]), "dl", 16)
+    lw = []
+    for i in range(4):
+        a, b = 1024 * i, 1024 * i + 1024
+        lw.append(run("ysys"[i], [], lambda q: q.dma_start(T.wt[:, a:b], T.w[:, a:b]), "dw%d" % i, 16))
+    for i in range(8):
+        lm = run("y", [], lambda q: q.dma_start(T.ml[16 * i:16 * i + 16, :], T.mp[:]), "dm", 16)
+
+    one = {}
+
+    def ones(m):
+        n = m * max(b - a for j, (a, b) in enumerate(CUT) if MAPS - len(VM[j]) == m)
+        d = run("v", [], lambda q: q.memset(T["one%d" % m][:, 0:n], 1.0))
+        one[m] = run("v", [d], lambda q: q.memset(T["one%d" % m][:, 0:n:m], 0.0))
+
+    for k in range(MAPS):
+        a = k * WIN + 1 + COLS + CAPP * r
+        run("v", [], lambda q: q.memset(T.win[:, a:a + CAPP], 0.0))
+    m3 = run("v", [], lambda q: q.memset(T.win[:, 0:MAPS * WIN:WIN], 0.0))
+    ones(MAPS - len(VM[0]))
+
+    c = CAPP // 16
+    for p in range(0, 128, 32):
+        so = run("v", [ll], lambda q: q.tensor_scalar(T.so[p:p + 32, :], T.sl[0:32, :], 0.0, 4.0,
+                                                      AluOpType.max, AluOpType.mult))
+
+    def gather(to, d, n):
+        for t in (0, 1):
+            o = [T.h[:, 4 * to + u:4 * (to + CAPP * n):4] for u in (t, t + 2)]
+            i = [T.xs[:, u:4 * COLS].indirect(T.so[:, c * d:c * (d + n)]) for u in (t, t + 2)]
+            v = run("v", [so, lx], lambda q: q.tensor_copy(o[0], i[0]))
+            s = run("s", [so, lx], lambda q: q.activation(o[1], i[1], Copy))
+        return [v, s]
+
+    used, total = [], [0]
+
+    def address(d, n):
+        e = [e for e in topo.engines(core, cores[d]) if e not in used][:n]
+        used.extend(e)
+        rid, pid = topo.addr(cores[d], core)
+        return {"dst_ids": [DstId(rid=rid, pnc=pid)], "dma_engine_mask": sum(1 << x for x in e),
+                "remote_sem": T.sem.near if d == near else T.sem.far}
+
+    def place(d):
+        return NEAR0 if d == near else FAR0 + CAPP * far_of(d).index(r)
+
+    def send(ranks, to, q, s, first):
+        for src, dst, codes in ((q, T.qf, True), (s, T.sf, False)):
+            out = []
+            for i, d in enumerate(ranks):
+                a, b = first + CAPP * i, place(d)
+                a, b = src[:, a:a + CAPP], dst[:, b:b + CAPP]
+                if codes:
+                    a, b = a.bitcast(dt.uint8), b.bitcast(dt.uint8)
+                out.append(RemoteDMATransfer(srcs=[a], dsts=[b], **to[i]))
+            g.remote_dma_fused(out, local_sem=T.sem.gone)
+
+    to = [address(d, 4) for d in far]
+    hf = gather(0, far[0], 2)
+    qh = run("v", hf, lambda q: q.quantize_mx(T.hq[:], T.hs[:], T.h[:, 0:8 * CAPP]))
+    wait("g", [qh])
+    send(far, to, T.hq, T.hs, 0)
+    hn = gather(2 * CAPP, near, 1)
+    qh = run("v", hf + hn, lambda q: q.quantize_mx(T.nq[:], T.ns[:], T.h[:, 4 * (3 * CAPP - 128):12 * CAPP]))
+    wait("g", [qh])
+    send([near], [address(near, NE)], T.nq, T.ns, 128 - CAPP)
+    arrived = [("near", 2 * NE), ("far", 2 * 8)]
+    wait("g", [("gone", 2 * len(used))])
+
+    qx = run("v", [lx], lambda q: q.quantize_mx(T.qf[:, 0:COLS], T.sf[:, 0:COLS], T.xs[:]))
+    qw = []
+    for i in range(4):
+        a, b = 256 * i, 256 * i + 256
+        qw.append(run("v", [lw[i]], lambda q: q.quantize_mx(T.qw[:, a:b], T.sw[:, a:b], T.wt[:, 4 * a:4 * b])))
+        if i == 1:
+            for m in sorted({MAPS - len(v) for v in VM} - set(one)):
+                ones(m)
+
+    def product(k, a, b, deps):
+        return run("t", [qw[k // 2]] + deps, lambda q: q.matmul_mx(
+            T.ps[:, 512 * k:512 * k + b - a], T.qw[:, 128 * k:128 * k + 128], T.sw[:, 128 * k:128 * k + 128],
+            T.qf[:, a:b], T.sf[:, a:b], True, True))
+
+    def keep(q, k, a, b, to, dep):
+        o, i = T.win[:, k * WIN + to:k * WIN + to + b - a], T.ps[:, 512 * k + a:512 * k + b]
+        if q == "v":
+            return run("v", [dep], lambda e: e.tensor_copy(o, i))
+        return run("s", [dep], lambda e: e.activation(o, i, Copy))
+
+    own = [product(k, 0, COLS, [qx]) for k in range(MAPS)]
+    ev = [keep("sv"[k % 2], k, 0, COLS, 1, own[k]) for k in range(MAPS)]
+    mo = run("v", [lm], lambda q: q.tensor_scalar(T.mo[:], T.ml[:], 1.0, None, add))
+    fr = [product(k, COLS, COLS + 3 * CAPP, [ev[k]] + arrived) for k in range(MAPS)]
+    done, got = {}, {}
+    base = [m3, mo]
+
+    def evac(q, k):
+        first = keep(q, k, 0, CAPP, 1 + COLS + CAPP * near, fr[k])
+        done[k] = [ev[k], first, keep(q, k, CAPP, 3 * CAPP, 1 + COLS + CAPP * far[0], fr[k])]
+
+    def pick(k, j):
+        a, b = CUT[j]
+        return T.win[:, k * WIN:k * WIN + WIN].indirect(T.mo[:, 32 * k + a // 16:32 * k + b // 16])
+
+    def spot(i, j):
+        a, b = CUT[j]
+        m = MAPS - len(VM[j])
+        return T.pq[:, 8 * a + i:8 * a + m * (b - a):m]
+
+    def spick(k, j):
+        sm = [x for x in range(MAPS) if x not in VM[j]]
+        i, (a, b) = sm.index(k), CUT[j]
+        o = T.gs[:, COLS * i + a:COLS * i + b] if i < len(VM[j]) - 1 else spot(i, j)
+        got[k, j] = run("s", base + done[k], lambda q: q.activation(o, pick(k, j), Copy))
+
+    def vpick(k, j):
+        sm = [x for x in range(MAPS) if x not in VM[j]]
+        i, (a, b) = VM[j].index(k), CUT[j]
+        got[k, j] = run("v", base + done[k] + [got[sm[i], j]], lambda q: q.tensor_tensor(
+            spot(i, j), pick(k, j), T.gs[:, COLS * i + a:COLS * i + b], add))
+
+    def finish(j):
+        k, (a, b) = VM[j][-1], CUT[j]
+        m = MAPS - len(VM[j])
+        z = run("v", base + [one[m]] + [got[x, j] for x in range(MAPS) if x != k], lambda q: q.tensor_tensor_scan(
+            T.zz[:, 8 * a:8 * a + m * (b - a)], T["one%d" % m][:, 0:m * (b - a)], T.pq[:, 8 * a:8 * a + m * (b - a)],
+            0.0, AluOpType.mult, add))
+        v = run("v", [z] + done[k], lambda q: q.tensor_tensor(
+            T.ys[:, a:b], pick(k, j), T.zz[:, 8 * a + m - 1:8 * a + m * (b - a):m], add))
+        got["y", j] = run("y", [v], lambda q: q.dma_start(T.y[:, a:b], T.ys[:, a:b]), "dy", 16)
+
+    todo = {"s": [], "v": []}
+    for j in range(len(CUT)):
+        sm = [x for x in range(MAPS) if x not in VM[j]]
+        for k in range(MAPS):
+            if j == 0:
+                q = "v" if k in EVV else "s"
+                todo[q].append((evac, (q, k), [], k))
+            if k in sm:
+                todo["s"].append((spick, (k, j), [k], (k, j)))
+            elif k != VM[j][-1]:
+                todo["v"].append((vpick, (k, j), [k, (sm[VM[j].index(k)], j)], (k, j)))
+        todo["v"].append((finish, (j,), list(range(MAPS)) + [(x, j) for x in range(MAPS) if x != VM[j][-1]], ("y", j)))
+    have = set()
+    while todo["s"] or todo["v"]:
+        for q in "sv":
+            while todo[q] and all(x in have for x in todo[q][0][2]):
+                f, args, _, made = todo[q].pop(0)
+                f(*args)
+                have.add(made)
+    wait("y", [got["y", len(CUT) - 1]])

@@ -4,10 +4,18 @@ from concourse.mybir import dt, AluOpType, ActivationFunctionType
 COLS, MAPS, CAPP, N = 512, 8, 96, 4
 WIN = 1 + COLS + N * CAPP
 NEAR0, FAR0 = COLS, COLS + CAPP
-CUT = [(0, 256), (256, 416), (416, 512)]
-VM = [[1, 3, 5, 7], [1, 7], [1, 7]]
-EVV = [1, 3, 5, 7]
 NE = 8
+CUT = [(0, 96), (96, 416), (416, 512)]
+VM = [[2, 6], [2, 1, 3, 4, 6, 5, 7], [0, 7]]
+ORDER = {
+    "v": [("E", 0), ("E", 1), ("E", 2), ("P", 2, 1), ("P", 1, 1), ("P", 3, 1), ("P", 4, 1), ("P", 0, 2), ("P", 6, 1), ("P", 5, 1),
+          ("Z", 2), ("F", 1), ("P", 2, 0), ("Z", 0), ("F", 2), ("F", 0)],
+    "s": [("P", 0, 1), ("E", 3), ("E", 4), ("P", 2, 2), ("P", 3, 2), ("P", 4, 2), ("E", 6), ("E", 5), ("P", 5, 2), ("P", 1, 2),
+          ("P", 0, 0), ("P", 6, 2), ("E", 7), ("P", 5, 0), ("P", 4, 0), ("P", 7, 0), ("P", 1, 0), ("P", 3, 0)],
+}
+SM = [[x[1] for x in ORDER["s"] if x[0] == "P" and x[2] == j] for j in range(len(CUT))]
+VOWN = [2, 5]
+TERMS = 6
 
 SCRATCH = {
     "xs": ("sbuf", [128, 4 * COLS], "bfloat16"),
@@ -26,15 +34,15 @@ SCRATCH = {
     "qw": ("sbuf", [128, 128 * MAPS], "float8_e4m3fn_x4"),
     "sw": ("sbuf", [128, 128 * MAPS], "uint8"),
     "win": ("sbuf", [128, MAPS * WIN], "float32"),
-    "gs": ("sbuf", [128, 3 * COLS], "float32"),
-    "pq": ("sbuf", [128, 8 * COLS], "float32"),
-    "zz": ("sbuf", [128, 8 * COLS], "float32"),
+    "gs": ("sbuf", [128, 2 * COLS], "float32"),
+    "vs": ("sbuf", [128, MAPS * COLS], "float32"),
+    "pq": ("sbuf", [128, TERMS * COLS], "float32"),
+    "zz": ("sbuf", [128, TERMS * COLS], "float32"),
     "ys": ("sbuf", [128, COLS], "float32"),
+    "one": ("sbuf", [128, TERMS * 128], "bfloat16"),
     "ps": ("psum", [128, 512 * MAPS], "float32"),
 }
-for _v in VM:
-    SCRATCH["one%d" % (MAPS - len(_v))] = ("sbuf", [128, 1024], "bfloat16")
-SEMAPHORES = ["v", "s", "t", "dx", "dl", "dw0", "dw1", "dw2", "dw3", "dm", "dy", "near", "far", "gone"]
+SEMAPHORES = ["v", "s", "t", "dx", "dl", "dw0", "dw1", "dm", "dy", "near", "far", "gone"]
 
 
 def rank_program(g, core, T, topo):
@@ -73,39 +81,37 @@ def rank_program(g, core, T, topo):
     lx = run("y", [], lambda q: q.dma_start(T.xs[32:128, :], T.x[32:128, :]), "dx", 16)
     ll = run("s", [], lambda q: q.dma_start(T.sl[16:32, :], T.send[:]), "dl", 16)
     lw = []
-    for i in range(4):
-        a, b = 1024 * i, 1024 * i + 1024
-        lw.append(run("ysys"[i], [], lambda q: q.dma_start(T.wt[:, a:b], T.w[:, a:b]), "dw%d" % i, 16))
+    for i in range(2):
+        a, b = 2048 * i, 2048 * i + 2048
+        lw.append(run("s", [], lambda q: q.dma_start(T.wt[:, a:b], T.w[:, a:b]), "dw%d" % i, 16))
     for i in range(8):
-        lm = run("y", [], lambda q: q.dma_start(T.ml[16 * i:16 * i + 16, :], T.mp[:]), "dm", 16)
-
-    one = {}
-
-    def ones(m):
-        n = m * max(b - a for j, (a, b) in enumerate(CUT) if MAPS - len(VM[j]) == m)
-        d = run("v", [], lambda q: q.memset(T["one%d" % m][:, 0:n], 1.0))
-        one[m] = run("v", [d], lambda q: q.memset(T["one%d" % m][:, 0:n:m], 0.0))
+        lm = run("y", [lx], lambda q: q.dma_start(T.ml[16 * i:16 * i + 16, :], T.mp[:]), "dm", 16)
 
     for k in range(MAPS):
         a = k * WIN + 1 + COLS + CAPP * r
         run("v", [], lambda q: q.memset(T.win[:, a:a + CAPP], 0.0))
     m3 = run("v", [], lambda q: q.memset(T.win[:, 0:MAPS * WIN:WIN], 0.0))
-    ones(MAPS - len(VM[0]))
 
     c = CAPP // 16
     for p in range(0, 128, 32):
         so = run("v", [ll], lambda q: q.tensor_scalar(T.so[p:p + 32, :], T.sl[0:32, :], 0.0, 4.0,
                                                       AluOpType.max, AluOpType.mult))
+    n1 = TERMS * max(b - a for j, (a, b) in enumerate(CUT) if len(SM[j]) == TERMS)
+    one = run("v", [], lambda q: q.memset(T.one[:, 0:n1], 1.0))
+    one = run("v", [one], lambda q: q.memset(T.one[:, 0:n1:TERMS], 0.0))
 
-    def gather(to, d, n):
-        for t in (0, 1):
-            o = [T.h[:, 4 * to + u:4 * (to + CAPP * n):4] for u in (t, t + 2)]
-            i = [T.xs[:, u:4 * COLS].indirect(T.so[:, c * d:c * (d + n)]) for u in (t, t + 2)]
-            v = run("v", [so, lx], lambda q: q.tensor_copy(o[0], i[0]))
-            s = run("s", [so, lx], lambda q: q.activation(o[1], i[1], Copy))
-        return [v, s]
+    def gather(to, d, n, qs):
+        last = {}
+        for t, q in enumerate(qs):
+            o = T.h[:, 4 * to + t:4 * (to + CAPP * n):4]
+            i = T.xs[:, t:4 * COLS].indirect(T.so[:, c * d:c * (d + n)])
+            if q == "v":
+                last[q] = run("v", [so, lx], lambda e: e.tensor_copy(o, i))
+            else:
+                last[q] = run("s", [so, lx], lambda e: e.activation(o, i, Copy))
+        return list(last.values())
 
-    used, total = [], [0]
+    used = []
 
     def address(d, n):
         e = [e for e in topo.engines(core, cores[d]) if e not in used][:n]
@@ -129,25 +135,23 @@ def rank_program(g, core, T, topo):
             g.remote_dma_fused(out, local_sem=T.sem.gone)
 
     to = [address(d, 4) for d in far]
-    hf = gather(0, far[0], 2)
+    hf = gather(0, far[0], 2, "vsvs")
     qh = run("v", hf, lambda q: q.quantize_mx(T.hq[:], T.hs[:], T.h[:, 0:8 * CAPP]))
     wait("g", [qh])
     send(far, to, T.hq, T.hs, 0)
-    hn = gather(2 * CAPP, near, 1)
-    qh = run("v", hf + hn, lambda q: q.quantize_mx(T.nq[:], T.ns[:], T.h[:, 4 * (3 * CAPP - 128):12 * CAPP]))
-    wait("g", [qh])
-    send([near], [address(near, NE)], T.nq, T.ns, 128 - CAPP)
-    arrived = [("near", 2 * NE), ("far", 2 * 8)]
-    wait("g", [("gone", 2 * len(used))])
+    hn = gather(2 * CAPP, near, 1, "ssss")
 
     qx = run("v", [lx], lambda q: q.quantize_mx(T.qf[:, 0:COLS], T.sf[:, 0:COLS], T.xs[:]))
     qw = []
     for i in range(4):
+        if i == 2:
+            qh = run("v", hf + hn, lambda q: q.quantize_mx(T.nq[:], T.ns[:], T.h[:, 4 * (3 * CAPP - 128):12 * CAPP]))
+            wait("g", [qh])
+            send([near], [address(near, NE)], T.nq, T.ns, 128 - CAPP)
+            wait("g", [("gone", 2 * len(used))])
         a, b = 256 * i, 256 * i + 256
-        qw.append(run("v", [lw[i]], lambda q: q.quantize_mx(T.qw[:, a:b], T.sw[:, a:b], T.wt[:, 4 * a:4 * b])))
-        if i == 1:
-            for m in sorted({MAPS - len(v) for v in VM} - set(one)):
-                ones(m)
+        qw.append(run("v", [lw[i // 2]], lambda q: q.quantize_mx(T.qw[:, a:b], T.sw[:, a:b], T.wt[:, 4 * a:4 * b])))
+    arrived = [("near", 2 * NE), ("far", 2 * 8)]
 
     def product(k, a, b, deps):
         return run("t", [qw[k // 2]] + deps, lambda q: q.matmul_mx(
@@ -161,8 +165,8 @@ def rank_program(g, core, T, topo):
         return run("s", [dep], lambda e: e.activation(o, i, Copy))
 
     own = [product(k, 0, COLS, [qx]) for k in range(MAPS)]
-    ev = [keep("sv"[k % 2], k, 0, COLS, 1, own[k]) for k in range(MAPS)]
     mo = run("v", [lm], lambda q: q.tensor_scalar(T.mo[:], T.ml[:], 1.0, None, add))
+    ev = [keep("v" if k in VOWN else "s", k, 0, COLS, 1, own[k]) for k in range(MAPS)]
     fr = [product(k, COLS, COLS + 3 * CAPP, [ev[k]] + arrived) for k in range(MAPS)]
     done, got = {}, {}
     base = [m3, mo]
@@ -177,48 +181,61 @@ def rank_program(g, core, T, topo):
 
     def spot(i, j):
         a, b = CUT[j]
-        m = MAPS - len(VM[j])
-        return T.pq[:, 8 * a + i:8 * a + m * (b - a):m]
+        return T.pq[:, TERMS * a + i:TERMS * b:TERMS]
+
+    def side(buf, i, j):
+        a, b = CUT[j]
+        return buf[:, COLS * i + a:COLS * i + b]
 
     def spick(k, j):
-        sm = [x for x in range(MAPS) if x not in VM[j]]
-        i, (a, b) = sm.index(k), CUT[j]
-        o = T.gs[:, COLS * i + a:COLS * i + b] if i < len(VM[j]) - 1 else spot(i, j)
+        i = SM[j].index(k)
+        o = side(T.gs, i, j) if i < len(VM[j]) - 1 and (i < 1 or len(SM[j]) == TERMS) else spot(i, j)
         got[k, j] = run("s", base + done[k], lambda q: q.activation(o, pick(k, j), Copy))
 
     def vpick(k, j):
-        sm = [x for x in range(MAPS) if x not in VM[j]]
-        i, (a, b) = VM[j].index(k), CUT[j]
-        got[k, j] = run("v", base + done[k] + [got[sm[i], j]], lambda q: q.tensor_tensor(
-            spot(i, j), pick(k, j), T.gs[:, COLS * i + a:COLS * i + b], add))
+        i, m = VM[j].index(k), len(SM[j])
+        if i < m:
+            dep, more = got[SM[j][i], j], side(T.gs, i, j)
+        else:
+            dep, more = got[VM[j][i - m], j], side(T.vs, i - m, j)
+        o = spot(i, j) if m == TERMS else side(T.vs, i, j)
+        got[k, j] = run("v", base + done[k] + [dep], lambda q: q.tensor_tensor(o, pick(k, j), more, add))
+
+    def scan(j):
+        a, b = TERMS * CUT[j][0], TERMS * CUT[j][1]
+        got["z", j] = run("v", [one] + [got[k, j] for k in range(MAPS) if k != VM[j][-1]], lambda q: q.tensor_tensor_scan(
+            T.zz[:, a:b], T.one[:, 0:b - a], T.pq[:, a:b], 0.0, AluOpType.mult, add))
 
     def finish(j):
         k, (a, b) = VM[j][-1], CUT[j]
-        m = MAPS - len(VM[j])
-        z = run("v", base + [one[m]] + [got[x, j] for x in range(MAPS) if x != k], lambda q: q.tensor_tensor_scan(
-            T.zz[:, 8 * a:8 * a + m * (b - a)], T["one%d" % m][:, 0:m * (b - a)], T.pq[:, 8 * a:8 * a + m * (b - a)],
-            0.0, AluOpType.mult, add))
-        v = run("v", [z] + done[k], lambda q: q.tensor_tensor(
-            T.ys[:, a:b], pick(k, j), T.zz[:, 8 * a + m - 1:8 * a + m * (b - a):m], add))
+        if len(SM[j]) == TERMS:
+            dep, more = got["z", j], T.zz[:, TERMS * a + TERMS - 1:TERMS * b:TERMS]
+        else:
+            dep, more = got[VM[j][-2], j], side(T.vs, len(VM[j]) - 2, j)
+        v = run("v", base + done[k] + [dep], lambda q: q.tensor_tensor(T.ys[:, a:b], pick(k, j), more, add))
         got["y", j] = run("y", [v], lambda q: q.dma_start(T.y[:, a:b], T.ys[:, a:b]), "dy", 16)
 
-    todo = {"s": [], "v": []}
-    for j in range(len(CUT)):
-        sm = [x for x in range(MAPS) if x not in VM[j]]
-        for k in range(MAPS):
-            if j == 0:
-                q = "v" if k in EVV else "s"
-                todo[q].append((evac, (q, k), [], k))
-            if k in sm:
-                todo["s"].append((spick, (k, j), [k], (k, j)))
-            elif k != VM[j][-1]:
-                todo["v"].append((vpick, (k, j), [k, (sm[VM[j].index(k)], j)], (k, j)))
-        todo["v"].append((finish, (j,), list(range(MAPS)) + [(x, j) for x in range(MAPS) if x != VM[j][-1]], ("y", j)))
-    have = set()
+    def call(q, x):
+        if x[0] == "E":
+            return evac, (q, x[1]), []
+        j = x[-1]
+        before = [("P", k, j) for k in range(MAPS) if k != VM[j][-1]]
+        if x[0] == "Z":
+            return scan, (j,), before
+        if x[0] == "F":
+            return finish, (j,), [("E", VM[j][-1])] + ([("Z", j)] if len(SM[j]) == TERMS else before)
+        if q == "s":
+            return spick, (x[1], j), [("E", x[1])]
+        i = VM[j].index(x[1])
+        return vpick, (x[1], j), [("E", x[1])] + [("P", k, j) for k in SM[j][i:i + 1]]
+
+    todo, have = {"s": list(ORDER["s"]), "v": list(ORDER["v"])}, set()
     while todo["s"] or todo["v"]:
         for q in "sv":
-            while todo[q] and all(x in have for x in todo[q][0][2]):
-                f, args, _, made = todo[q].pop(0)
+            while todo[q]:
+                f, args, deps = call(q, todo[q][0])
+                if not all(x in have for x in deps):
+                    break
                 f(*args)
-                have.add(made)
-    wait("y", [got["y", len(CUT) - 1]])
+                have.add(todo[q].pop(0))
+    wait("y", [got["y", j] for j in (1, 2, 0)][-1:])

@@ -2,16 +2,16 @@ from concourse.bass import DstId, RemoteDMATransfer
 from concourse.mybir import dt, AluOpType, ActivationFunctionType
 
 COLS, MAPS, CAPP, N = 512, 8, 96, 4
-WIN = 1 + COLS + N * CAPP
-NEAR0, FAR0 = COLS, COLS + CAPP
+SLOTS = (N - 1) * CAPP
+WIN = 1 + COLS + SLOTS
 NE = 8
-CUT = [(0, 96), (96, 416), (416, 512)]
-VM = [[2, 6], [2, 1, 3, 4, 6, 5, 7], [0, 7]]
+CUT = [(0, 128), (128, 448), (448, 512)]
+VM = [[2, 7], [1, 2, 3, 4, 6, 5, 7], [5, 7]]
 ORDER = {
-    "v": [("E", 0), ("E", 1), ("E", 2), ("P", 2, 1), ("P", 1, 1), ("P", 3, 1), ("P", 4, 1), ("P", 0, 2), ("P", 6, 1), ("P", 5, 1),
-          ("Z", 2), ("F", 1), ("P", 2, 0), ("Z", 0), ("F", 2), ("F", 0)],
-    "s": [("P", 0, 1), ("E", 3), ("E", 4), ("P", 2, 2), ("P", 3, 2), ("P", 4, 2), ("E", 6), ("E", 5), ("P", 5, 2), ("P", 1, 2),
-          ("P", 0, 0), ("P", 6, 2), ("E", 7), ("P", 5, 0), ("P", 4, 0), ("P", 7, 0), ("P", 1, 0), ("P", 3, 0)],
+    "v": [("E", 0), ("E", 1), ("E", 2), ("P", 1, 1), ("P", 2, 1), ("P", 2, 0), ("P", 3, 1), ("P", 4, 1), ("P", 5, 2), ("P", 6, 1),
+          ("P", 5, 1), ("Z", 0), ("F", 1), ("Z", 2), ("F", 0), ("F", 2)],
+    "s": [("P", 0, 1), ("P", 1, 0), ("E", 3), ("E", 4), ("E", 5), ("E", 6), ("P", 0, 2), ("P", 6, 2), ("P", 4, 0), ("P", 5, 0),
+          ("P", 6, 0), ("P", 3, 0), ("P", 0, 0), ("P", 4, 2), ("P", 1, 2), ("P", 2, 2), ("E", 7), ("P", 3, 2)],
 }
 SM = [[x[1] for x in ORDER["s"] if x[0] == "P" and x[2] == j] for j in range(len(CUT))]
 VOWN = [2, 5]
@@ -23,14 +23,16 @@ SCRATCH = {
     "sl": ("sbuf", [32, N * CAPP // 16], "int32"),
     "so": ("sbuf", [128, N * CAPP // 16], "uint16"),
     "ml": ("sbuf", [128, MAPS * COLS // 16], "int32"),
+    "mt": ("sbuf", [128, MAPS * COLS // 16], "int32"),
+    "mu": ("sbuf", [128, MAPS * COLS // 16], "int32"),
     "mo": ("sbuf", [128, MAPS * COLS // 16], "uint16"),
-    "h": ("sbuf", [128, 4 * 3 * CAPP], "bfloat16"),
+    "h": ("sbuf", [128, 4 * SLOTS], "bfloat16"),
     "hq": ("sbuf", [128, 2 * CAPP], "float8_e4m3fn_x4"),
     "hs": ("sbuf", [128, 2 * CAPP], "uint8"),
     "nq": ("sbuf", [128, 128], "float8_e4m3fn_x4"),
     "ns": ("sbuf", [128, 128], "uint8"),
-    "qf": ("sbuf", [128, COLS + 3 * CAPP], "float8_e4m3fn_x4"),
-    "sf": ("sbuf", [128, COLS + 3 * CAPP], "uint8"),
+    "qf": ("sbuf", [128, COLS + SLOTS], "float8_e4m3fn_x4"),
+    "sf": ("sbuf", [128, COLS + SLOTS], "uint8"),
     "qw": ("sbuf", [128, 128 * MAPS], "float8_e4m3fn_x4"),
     "sw": ("sbuf", [128, 128 * MAPS], "uint8"),
     "win": ("sbuf", [128, MAPS * WIN], "float32"),
@@ -87,18 +89,15 @@ def rank_program(g, core, T, topo):
     for i in range(8):
         lm = run("y", [lx], lambda q: q.dma_start(T.ml[16 * i:16 * i + 16, :], T.mp[:]), "dm", 16)
 
-    for k in range(MAPS):
-        a = k * WIN + 1 + COLS + CAPP * r
-        run("v", [], lambda q: q.memset(T.win[:, a:a + CAPP], 0.0))
     m3 = run("v", [], lambda q: q.memset(T.win[:, 0:MAPS * WIN:WIN], 0.0))
+    n1 = TERMS * max(b - a for j, (a, b) in enumerate(CUT) if len(SM[j]) == TERMS)
+    one = run("v", [], lambda q: q.memset(T.one[:, 0:n1], 1.0))
+    one = run("v", [one], lambda q: q.memset(T.one[:, 0:n1:TERMS], 0.0))
 
     c = CAPP // 16
     for p in range(0, 128, 32):
         so = run("v", [ll], lambda q: q.tensor_scalar(T.so[p:p + 32, :], T.sl[0:32, :], 0.0, 4.0,
                                                       AluOpType.max, AluOpType.mult))
-    n1 = TERMS * max(b - a for j, (a, b) in enumerate(CUT) if len(SM[j]) == TERMS)
-    one = run("v", [], lambda q: q.memset(T.one[:, 0:n1], 1.0))
-    one = run("v", [one], lambda q: q.memset(T.one[:, 0:n1:TERMS], 0.0))
 
     def gather(to, d, n, qs):
         last = {}
@@ -121,7 +120,7 @@ def rank_program(g, core, T, topo):
                 "remote_sem": T.sem.near if d == near else T.sem.far}
 
     def place(d):
-        return NEAR0 if d == near else FAR0 + CAPP * far_of(d).index(r)
+        return COLS + CAPP * [s for s in range(N) if s != d].index(r)
 
     def send(ranks, to, q, s, first):
         for src, dst, codes in ((q, T.qf, True), (s, T.sf, False)):
@@ -145,7 +144,7 @@ def rank_program(g, core, T, topo):
     qw = []
     for i in range(4):
         if i == 2:
-            qh = run("v", hf + hn, lambda q: q.quantize_mx(T.nq[:], T.ns[:], T.h[:, 4 * (3 * CAPP - 128):12 * CAPP]))
+            qh = run("v", hf + hn, lambda q: q.quantize_mx(T.nq[:], T.ns[:], T.h[:, 4 * (SLOTS - 128):4 * SLOTS]))
             wait("g", [qh])
             send([near], [address(near, NE)], T.nq, T.ns, 128 - CAPP)
             wait("g", [("gone", 2 * len(used))])
@@ -158,22 +157,24 @@ def rank_program(g, core, T, topo):
             T.ps[:, 512 * k:512 * k + b - a], T.qw[:, 128 * k:128 * k + 128], T.sw[:, 128 * k:128 * k + 128],
             T.qf[:, a:b], T.sf[:, a:b], True, True))
 
-    def keep(q, k, a, b, to, dep):
-        o, i = T.win[:, k * WIN + to:k * WIN + to + b - a], T.ps[:, 512 * k + a:512 * k + b]
+    def keep(q, k, n, to, dep):
+        o, i = T.win[:, k * WIN + to:k * WIN + to + n], T.ps[:, 512 * k:512 * k + n]
         if q == "v":
             return run("v", [dep], lambda e: e.tensor_copy(o, i))
         return run("s", [dep], lambda e: e.activation(o, i, Copy))
 
     own = [product(k, 0, COLS, [qx]) for k in range(MAPS)]
-    mo = run("v", [lm], lambda q: q.tensor_scalar(T.mo[:], T.ml[:], 1.0, None, add))
-    ev = [keep("v" if k in VOWN else "s", k, 0, COLS, 1, own[k]) for k in range(MAPS)]
-    fr = [product(k, COLS, COLS + 3 * CAPP, [ev[k]] + arrived) for k in range(MAPS)]
+    mt = run("v", [lm], lambda q: q.tensor_scalar(T.mt[:], T.ml[:], float(COLS + CAPP * (r + 1)), float(-CAPP),
+                                                  AluOpType.is_ge, AluOpType.mult))
+    mu = run("v", [mt, lm], lambda q: q.tensor_tensor(T.mu[:], T.ml[:], T.mt[:], add))
+    mo = run("v", [mu], lambda q: q.tensor_scalar(T.mo[:], T.mu[:], 1.0, None, add))
+    ev = [keep("v" if k in VOWN else "s", k, COLS, 1, own[k]) for k in range(MAPS)]
+    fr = [product(k, COLS, COLS + SLOTS, [ev[k]] + arrived) for k in range(MAPS)]
     done, got = {}, {}
     base = [m3, mo]
 
     def evac(q, k):
-        first = keep(q, k, 0, CAPP, 1 + COLS + CAPP * near, fr[k])
-        done[k] = [ev[k], first, keep(q, k, CAPP, 3 * CAPP, 1 + COLS + CAPP * far[0], fr[k])]
+        done[k] = [ev[k], keep(q, k, SLOTS, 1 + COLS, fr[k])]
 
     def pick(k, j):
         a, b = CUT[j]
@@ -189,16 +190,16 @@ def rank_program(g, core, T, topo):
 
     def spick(k, j):
         i = SM[j].index(k)
-        o = side(T.gs, i, j) if i < len(VM[j]) - 1 and (i < 1 or len(SM[j]) == TERMS) else spot(i, j)
+        o = side(T.gs, 0, j) if i == 0 else spot(i, j)
         got[k, j] = run("s", base + done[k], lambda q: q.activation(o, pick(k, j), Copy))
 
     def vpick(k, j):
-        i, m = VM[j].index(k), len(SM[j])
-        if i < m:
-            dep, more = got[SM[j][i], j], side(T.gs, i, j)
+        i = VM[j].index(k)
+        if i == 0:
+            dep, more = got[SM[j][0], j], side(T.gs, 0, j)
         else:
-            dep, more = got[VM[j][i - m], j], side(T.vs, i - m, j)
-        o = spot(i, j) if m == TERMS else side(T.vs, i, j)
+            dep, more = got[VM[j][i - 1], j], side(T.vs, i - 1, j)
+        o = spot(i, j) if len(SM[j]) == TERMS else side(T.vs, i, j)
         got[k, j] = run("v", base + done[k] + [dep], lambda q: q.tensor_tensor(o, pick(k, j), more, add))
 
     def scan(j):
@@ -213,7 +214,7 @@ def rank_program(g, core, T, topo):
         else:
             dep, more = got[VM[j][-2], j], side(T.vs, len(VM[j]) - 2, j)
         v = run("v", base + done[k] + [dep], lambda q: q.tensor_tensor(T.ys[:, a:b], pick(k, j), more, add))
-        got["y", j] = run("y", [v], lambda q: q.dma_start(T.y[:, a:b], T.ys[:, a:b]), "dy", 16)
+        got["y"] = run("y", [v], lambda q: q.dma_start(T.y[:, a:b], T.ys[:, a:b]), "dy", 16)
 
     def call(q, x):
         if x[0] == "E":
@@ -226,8 +227,7 @@ def rank_program(g, core, T, topo):
             return finish, (j,), [("E", VM[j][-1])] + ([("Z", j)] if len(SM[j]) == TERMS else before)
         if q == "s":
             return spick, (x[1], j), [("E", x[1])]
-        i = VM[j].index(x[1])
-        return vpick, (x[1], j), [("E", x[1])] + [("P", k, j) for k in SM[j][i:i + 1]]
+        return vpick, (x[1], j), [("E", x[1])] + ([("P", SM[j][0], j)] if VM[j][0] == x[1] else [])
 
     todo, have = {"s": list(ORDER["s"]), "v": list(ORDER["v"])}, set()
     while todo["s"] or todo["v"]:
@@ -238,4 +238,4 @@ def rank_program(g, core, T, topo):
                     break
                 f(*args)
                 have.add(todo[q].pop(0))
-    wait("y", [got["y", j] for j in (1, 2, 0)][-1:])
+    wait("y", [got["y"]])

from concourse.bass import DstId, RemoteDMATransfer
from concourse.mybir import dt, AluOpType, ActivationFunctionType

COLS, MAPS, CAPP, N = 512, 8, 96, 4
SLOTS = (N - 1) * CAPP
WIN = 1 + COLS + SLOTS
NE = 8
CUT = [(0, 128), (128, 448), (448, 512)]
VM = [[2, 7], [1, 2, 3, 4, 6, 5, 7], [5, 7]]
ORDER = {
    "v": [("E", 0), ("E", 1), ("E", 2), ("P", 1, 1), ("P", 2, 1), ("P", 2, 0), ("P", 3, 1), ("P", 4, 1), ("P", 5, 2), ("P", 6, 1),
          ("P", 5, 1), ("Z", 0), ("F", 1), ("Z", 2), ("F", 0), ("F", 2)],
    "s": [("P", 0, 1), ("P", 1, 0), ("E", 3), ("E", 4), ("E", 5), ("E", 6), ("P", 0, 2), ("P", 6, 2), ("P", 4, 0), ("P", 5, 0),
          ("P", 6, 0), ("P", 3, 0), ("P", 0, 0), ("P", 4, 2), ("P", 1, 2), ("P", 2, 2), ("E", 7), ("P", 3, 2)],
}
SM = [[x[1] for x in ORDER["s"] if x[0] == "P" and x[2] == j] for j in range(len(CUT))]
VOWN = [2, 5]
TERMS = 6

SCRATCH = {
    "xs": ("sbuf", [128, 4 * COLS], "bfloat16"),
    "wt": ("sbuf", [128, 512 * MAPS], "bfloat16"),
    "sl": ("sbuf", [32, N * CAPP // 16], "int32"),
    "so": ("sbuf", [128, N * CAPP // 16], "uint16"),
    "ml": ("sbuf", [128, MAPS * COLS // 16], "int32"),
    "mt": ("sbuf", [128, MAPS * COLS // 16], "int32"),
    "mu": ("sbuf", [128, MAPS * COLS // 16], "int32"),
    "mo": ("sbuf", [128, MAPS * COLS // 16], "uint16"),
    "h": ("sbuf", [128, 4 * SLOTS], "bfloat16"),
    "hq": ("sbuf", [128, 2 * CAPP], "float8_e4m3fn_x4"),
    "hs": ("sbuf", [128, 2 * CAPP], "uint8"),
    "nq": ("sbuf", [128, 128], "float8_e4m3fn_x4"),
    "ns": ("sbuf", [128, 128], "uint8"),
    "qf": ("sbuf", [128, COLS + SLOTS], "float8_e4m3fn_x4"),
    "sf": ("sbuf", [128, COLS + SLOTS], "uint8"),
    "qw": ("sbuf", [128, 128 * MAPS], "float8_e4m3fn_x4"),
    "sw": ("sbuf", [128, 128 * MAPS], "uint8"),
    "win": ("sbuf", [128, MAPS * WIN], "float32"),
    "gs": ("sbuf", [128, 2 * COLS], "float32"),
    "vs": ("sbuf", [128, MAPS * COLS], "float32"),
    "pq": ("sbuf", [128, TERMS * COLS], "float32"),
    "zz": ("sbuf", [128, TERMS * COLS], "float32"),
    "ys": ("sbuf", [128, COLS], "float32"),
    "one": ("sbuf", [128, TERMS * 128], "bfloat16"),
    "ps": ("psum", [128, 512 * MAPS], "float32"),
}
SEMAPHORES = ["v", "s", "t", "dx", "dl", "dw0", "dw1", "dm", "dy", "near", "far", "gone"]


def rank_program(g, core, T, topo):
    r = T.rank_of(core)
    if r is None:
        return
    cores = list(T.cores)

    def near_of(d):
        return [s for s in range(N) if s != d and cores[s] in topo.cores_of(cores[d])]

    def far_of(d):
        return [s for s in range(N) if cores[s] not in topo.cores_of(cores[d])]

    near, far = near_of(r)[0], far_of(r)
    Copy, add = ActivationFunctionType.Copy, AluOpType.add

    queue = {"v": g.vector, "s": g.scalar, "t": g.tensor, "y": g.sync, "g": g}
    count, seen = {}, {}

    def wait(q, deps):
        for sem, n in deps:
            if seen.get((q, sem), 0) < n:
                queue[q].wait_ge(T.sem[sem], n)
                seen[(q, sem)] = n

    def run(q, deps, call, sem=None, n=1):
        wait(q, deps)
        sem = sem or q
        call(queue[q]).then_inc(T.sem[sem], n)
        count[sem] = count.get(sem, 0) + n
        return (sem, count[sem])

    run("y", [], lambda q: q.dma_start(T.xs[0:32, :], T.x[0:32, :]), "dx", 16)
    run("s", [], lambda q: q.dma_start(T.sl[0:16, :], T.send[:]), "dl", 16)
    lx = run("y", [], lambda q: q.dma_start(T.xs[32:128, :], T.x[32:128, :]), "dx", 16)
    ll = run("s", [], lambda q: q.dma_start(T.sl[16:32, :], T.send[:]), "dl", 16)
    lw = []
    for i in range(2):
        a, b = 2048 * i, 2048 * i + 2048
        lw.append(run("s", [], lambda q: q.dma_start(T.wt[:, a:b], T.w[:, a:b]), "dw%d" % i, 16))
    for i in range(8):
        lm = run("y", [lx], lambda q: q.dma_start(T.ml[16 * i:16 * i + 16, :], T.mp[:]), "dm", 16)

    m3 = run("v", [], lambda q: q.memset(T.win[:, 0:MAPS * WIN:WIN], 0.0))
    n1 = TERMS * max(b - a for j, (a, b) in enumerate(CUT) if len(SM[j]) == TERMS)
    one = run("v", [], lambda q: q.memset(T.one[:, 0:n1], 1.0))
    one = run("v", [one], lambda q: q.memset(T.one[:, 0:n1:TERMS], 0.0))

    c = CAPP // 16
    for p in range(0, 128, 32):
        so = run("v", [ll], lambda q: q.tensor_scalar(T.so[p:p + 32, :], T.sl[0:32, :], 0.0, 4.0,
                                                      AluOpType.max, AluOpType.mult))

    def gather(to, d, n, qs):
        last = {}
        for t, q in enumerate(qs):
            o = T.h[:, 4 * to + t:4 * (to + CAPP * n):4]
            i = T.xs[:, t:4 * COLS].indirect(T.so[:, c * d:c * (d + n)])
            if q == "v":
                last[q] = run("v", [so, lx], lambda e: e.tensor_copy(o, i))
            else:
                last[q] = run("s", [so, lx], lambda e: e.activation(o, i, Copy))
        return list(last.values())

    used = []

    def address(d, n):
        e = [e for e in topo.engines(core, cores[d]) if e not in used][:n]
        used.extend(e)
        rid, pid = topo.addr(cores[d], core)
        return {"dst_ids": [DstId(rid=rid, pnc=pid)], "dma_engine_mask": sum(1 << x for x in e),
                "remote_sem": T.sem.near if d == near else T.sem.far}

    def place(d):
        return COLS + CAPP * [s for s in range(N) if s != d].index(r)

    def send(ranks, to, q, s, first):
        for src, dst, codes in ((q, T.qf, True), (s, T.sf, False)):
            out = []
            for i, d in enumerate(ranks):
                a, b = first + CAPP * i, place(d)
                a, b = src[:, a:a + CAPP], dst[:, b:b + CAPP]
                if codes:
                    a, b = a.bitcast(dt.uint8), b.bitcast(dt.uint8)
                out.append(RemoteDMATransfer(srcs=[a], dsts=[b], **to[i]))
            g.remote_dma_fused(out, local_sem=T.sem.gone)

    to = [address(d, 4) for d in far]
    hf = gather(0, far[0], 2, "vsvs")
    qh = run("v", hf, lambda q: q.quantize_mx(T.hq[:], T.hs[:], T.h[:, 0:8 * CAPP]))
    wait("g", [qh])
    send(far, to, T.hq, T.hs, 0)
    hn = gather(2 * CAPP, near, 1, "ssss")

    qx = run("v", [lx], lambda q: q.quantize_mx(T.qf[:, 0:COLS], T.sf[:, 0:COLS], T.xs[:]))
    qw = []
    for i in range(4):
        if i == 2:
            qh = run("v", hf + hn, lambda q: q.quantize_mx(T.nq[:], T.ns[:], T.h[:, 4 * (SLOTS - 128):4 * SLOTS]))
            wait("g", [qh])
            send([near], [address(near, NE)], T.nq, T.ns, 128 - CAPP)
            wait("g", [("gone", 2 * len(used))])
        a, b = 256 * i, 256 * i + 256
        qw.append(run("v", [lw[i // 2]], lambda q: q.quantize_mx(T.qw[:, a:b], T.sw[:, a:b], T.wt[:, 4 * a:4 * b])))
    arrived = [("near", 2 * NE), ("far", 2 * 8)]

    def product(k, a, b, deps):
        return run("t", [qw[k // 2]] + deps, lambda q: q.matmul_mx(
            T.ps[:, 512 * k:512 * k + b - a], T.qw[:, 128 * k:128 * k + 128], T.sw[:, 128 * k:128 * k + 128],
            T.qf[:, a:b], T.sf[:, a:b], True, True))

    def keep(q, k, n, to, dep):
        o, i = T.win[:, k * WIN + to:k * WIN + to + n], T.ps[:, 512 * k:512 * k + n]
        if q == "v":
            return run("v", [dep], lambda e: e.tensor_copy(o, i))
        return run("s", [dep], lambda e: e.activation(o, i, Copy))

    own = [product(k, 0, COLS, [qx]) for k in range(MAPS)]
    mt = run("v", [lm], lambda q: q.tensor_scalar(T.mt[:], T.ml[:], float(COLS + CAPP * (r + 1)), float(-CAPP),
                                                  AluOpType.is_ge, AluOpType.mult))
    mu = run("v", [mt, lm], lambda q: q.tensor_tensor(T.mu[:], T.ml[:], T.mt[:], add))
    mo = run("v", [mu], lambda q: q.tensor_scalar(T.mo[:], T.mu[:], 1.0, None, add))
    ev = [keep("v" if k in VOWN else "s", k, COLS, 1, own[k]) for k in range(MAPS)]
    fr = [product(k, COLS, COLS + SLOTS, [ev[k]] + arrived) for k in range(MAPS)]
    done, got = {}, {}
    base = [m3, mo]

    def evac(q, k):
        done[k] = [ev[k], keep(q, k, SLOTS, 1 + COLS, fr[k])]

    def pick(k, j):
        a, b = CUT[j]
        return T.win[:, k * WIN:k * WIN + WIN].indirect(T.mo[:, 32 * k + a // 16:32 * k + b // 16])

    def spot(i, j):
        a, b = CUT[j]
        return T.pq[:, TERMS * a + i:TERMS * b:TERMS]

    def side(buf, i, j):
        a, b = CUT[j]
        return buf[:, COLS * i + a:COLS * i + b]

    def spick(k, j):
        i = SM[j].index(k)
        o = side(T.gs, 0, j) if i == 0 else spot(i, j)
        got[k, j] = run("s", base + done[k], lambda q: q.activation(o, pick(k, j), Copy))

    def vpick(k, j):
        i = VM[j].index(k)
        if i == 0:
            dep, more = got[SM[j][0], j], side(T.gs, 0, j)
        else:
            dep, more = got[VM[j][i - 1], j], side(T.vs, i - 1, j)
        o = spot(i, j) if len(SM[j]) == TERMS else side(T.vs, i, j)
        got[k, j] = run("v", base + done[k] + [dep], lambda q: q.tensor_tensor(o, pick(k, j), more, add))

    def scan(j):
        a, b = TERMS * CUT[j][0], TERMS * CUT[j][1]
        got["z", j] = run("v", [one] + [got[k, j] for k in range(MAPS) if k != VM[j][-1]], lambda q: q.tensor_tensor_scan(
            T.zz[:, a:b], T.one[:, 0:b - a], T.pq[:, a:b], 0.0, AluOpType.mult, add))

    def finish(j):
        k, (a, b) = VM[j][-1], CUT[j]
        if len(SM[j]) == TERMS:
            dep, more = got["z", j], T.zz[:, TERMS * a + TERMS - 1:TERMS * b:TERMS]
        else:
            dep, more = got[VM[j][-2], j], side(T.vs, len(VM[j]) - 2, j)
        v = run("v", base + done[k] + [dep], lambda q: q.tensor_tensor(T.ys[:, a:b], pick(k, j), more, add))
        got["y"] = run("y", [v], lambda q: q.dma_start(T.y[:, a:b], T.ys[:, a:b]), "dy", 16)

    def call(q, x):
        if x[0] == "E":
            return evac, (q, x[1]), []
        j = x[-1]
        before = [("P", k, j) for k in range(MAPS) if k != VM[j][-1]]
        if x[0] == "Z":
            return scan, (j,), before
        if x[0] == "F":
            return finish, (j,), [("E", VM[j][-1])] + ([("Z", j)] if len(SM[j]) == TERMS else before)
        if q == "s":
            return spick, (x[1], j), [("E", x[1])]
        return vpick, (x[1], j), [("E", x[1])] + ([("P", SM[j][0], j)] if VM[j][0] == x[1] else [])

    todo, have = {"s": list(ORDER["s"]), "v": list(ORDER["v"])}, set()
    while todo["s"] or todo["v"]:
        for q in "sv":
            while todo[q]:
                f, args, deps = call(q, todo[q][0])
                if not all(x in have for x in deps):
                    break
                f(*args)
                have.add(todo[q].pop(0))
    wait("y", [got["y"]])
